import numpy as np
import ml_dtypes


def mxq(x, axis, fmt="e4m3"):
    dtype, down = {"e4m3": (ml_dtypes.float8_e4m3fn, 7), "e5m2": (ml_dtypes.float8_e5m2, 14)}[fmt]
    v = np.moveaxis(np.asarray(x, np.float32).astype(ml_dtypes.bfloat16).astype(np.float64), axis, -1)
    blocks = v.reshape(v.shape[:-1] + (-1, 32))
    amax = np.abs(blocks).max(-1, keepdims=True)
    byte = np.maximum(np.where(amax > 0, np.frexp(amax)[1] - 1 + 127, 0) - down, 1)
    scale = np.exp2(byte - 127.0)
    codes = (blocks / scale).astype(np.float32).astype(dtype).astype(np.float64)
    return np.moveaxis((codes * scale).reshape(v.shape), -1, axis)


WIDE = False


def mx_kscale(k):
    if not WIDE:
        return np.ones(k)
    levels = np.array([30, -30])
    if k % 512:
        return np.exp2(np.random.permutation(np.resize(levels, k // 32))).repeat(32)
    a = np.empty((k // 512, 16))
    for p in range(k // 512):
        a[p, :8] = np.random.permutation(np.resize(levels, 8))
        for g in range(8):
            far = levels[np.abs(levels - a[p, g]) >= 10]
            a[p, g + 8] = far[np.random.randint(len(far))]
    return np.exp2(a.ravel()).repeat(32)


def f64(x):
    return np.asarray(x).astype(np.float64)


def striped(idx):
    return np.tile(idx.reshape(-1, 16).T, (8, 1)).astype(np.uint16)


def unstriped(offs):
    return offs[:16].T.reshape(-1).astype(np.int64)


def d_relu2(v):
    return 2.0 * np.maximum(v, 0.0)


K, T, E, C, H, N = 128, 2560, 4, 512, 512, 512


def by_expert(wq, xq):
    return np.concatenate([wq[e].T @ xq[:, e * C:(e + 1) * C] for e in range(E)], axis=1)


def setup_inputs():
    n = np.random.standard_normal
    slot_token = np.random.permutation(T)[:E * C]
    s = mx_kscale(N)[:, None]
    z = np.ones(T); z[slot_token] = mx_kscale(E * C)
    return {
        "xT": (n((K, T)) * z[None, :]).astype(np.float32),
        "dyT": (n((N, T)) * s).astype(np.float32),
        "a": n((H, E * C)).astype(np.float32),
        "w2": (n((E, N, H)) / np.sqrt(N) / s[None]).astype(np.float32),
        "gate": np.tile(np.random.uniform(0.2, 1.0, E * C) / z[slot_token], (N, 1)).astype(np.float32),
        "offs": striped(slot_token),
    }


def reference(xT, dyT, a, w2, gate, offs):
    idx = unstriped(offs)
    gq = mxq(f64(gate) * f64(dyT)[:, idx], 0, "e5m2")
    dh = by_expert(mxq(f64(w2), 1, "e4m3"), gq)
    da = mxq(dh * d_relu2(f64(a)), 1, "e5m2")
    xq = mxq(f64(xT)[:, idx], 1, "e4m3")
    return np.stack([(xq[:, e * C:(e + 1) * C] @ da[:, e * C:(e + 1) * C].T) for e in range(E)])

@@ -1,0 +1,257 @@
+from contextlib import ExitStack
+
+import concourse.mybir as mybir
+from concourse.masks import make_identity
+
+K, T, E, C, H, N = 128, 2560, 4, 512, 512, 512
+S = E * C
+P = 128
+PACK = 4
+LIST_COL = 16
+
+FLOPS = 2 * S * N * H + 2 * S * K * H
+BYTES = 4 * (K * T + N * T + H * S + E * N * H + S + E * K * H) + 2 * P * (S // LIST_COL)
+
+F32 = mybir.dt.float32
+BF16 = mybir.dt.bfloat16
+U32 = mybir.dt.uint32
+U16 = mybir.dt.uint16
+U8 = mybir.dt.uint8
+E4M3 = mybir.dt.float8_e4m3fn_x4
+E5M2 = mybir.dt.float8_e5m2_x4
+MULT = mybir.AluOpType.mult
+MAX = mybir.AluOpType.max
+COPY = mybir.ActivationFunctionType.Copy
+
+
+def tile_moe_mlp_relu2_kernel(tc, xT, dyT, a, w2, gate, offs, out):
+    nc = tc.nc
+    with ExitStack() as ctx:
+        keep = ctx.enter_context(tc.tile_pool(name="keep", bufs=1))
+        ring = ctx.enter_context(tc.tile_pool(name="ring", bufs=2))
+        dh_psum = ctx.enter_context(tc.psum_pool(name="dh_psum", bufs=4))
+        turn_psum = ctx.enter_context(tc.psum_pool(name="turn_psum", bufs=2))
+        misc_psum = ctx.enter_context(tc.psum_pool(name="misc_psum", bufs=2))
+
+        offsets = keep.tile([P, S // LIST_COL], U16, name="offsets")
+        x_win = keep.tile([P, T], F32, name="x_win")
+        dy_win = [keep.tile([P, T], F32, name="dy_win%d" % j) for j in range(PACK)]
+        gate_sb = keep.tile([P, S], F32, name="gate_sb")
+        w_raw = [keep.tile([P, PACK, H], F32, name="w_raw%d" % e) for e in range(E)]
+        a_sb = [keep.tile([P, H // P, C], F32, name="a_sb%d" % e) for e in range(E)]
+        x_slots = keep.tile([P, S], F32, name="x_slots")
+        g_rows = keep.tile([P, PACK, S], F32, name="g_rows")
+        ident = keep.tile([P, P], F32, name="ident")
+        x_grouped = keep.tile([P, E, K, PACK], BF16, name="x_grouped", align_bytes=64)
+        x_codes = keep.tile([P, E * K], U32, name="x_codes", align_bytes=64)
+        x_scales = keep.tile([P, E * K], U8, name="x_scales", align_bytes=64)
+        w_codes = [keep.tile([P, H], U32, name="w_codes%d" % e, align_bytes=64) for e in range(E)]
+        w_scales = [keep.tile([P, H], U8, name="w_scales%d" % e, align_bytes=64) for e in range(E)]
+
+        dy_rows = dyT.rearrange("(p j) t -> j p t", j=PACK)
+        a_rows = a.rearrange("(b p) s -> p b s", p=P)
+
+        def load_dy(j):
+            nc.sync.dma_start(out=dy_win[j][:], in_=dy_rows[j])
+
+        def load_gate(lo, hi):
+            nc.sync.dma_start(out=gate_sb[:, lo:hi], in_=gate[0:P, lo:hi])
+
+        def load_w(e):
+            nc.sync.dma_start(out=w_raw[e][:], in_=w2[e].rearrange("(p j) i -> p j i", j=PACK))
+
+        def load_a(e):
+            nc.sync.dma_start(out=a_sb[e][:], in_=a_rows[:, :, e * C:(e + 1) * C])
+
+        def listed(lo, hi):
+            return offsets[:, lo // LIST_COL:hi // LIST_COL]
+
+        def gather_g(j, lo, hi):
+            nc.vector.tensor_tensor(g_rows[:, j, lo:hi], dy_win[j][:].indirect(listed(lo, hi)), gate_sb[:, lo:hi], MULT)
+
+        def interleave(dst, src):
+            nc.scalar.copy(
+                out=dst.rearrange("p (c i) j -> p c j i", i=4),
+                in_=src.rearrange("p j (c i) -> p c j i", i=4),
+            )
+
+        def quantize(codes, scales, grouped, fmt):
+            nc.vector.quantize_mx(out=codes.bitcast(fmt), scales=scales, in_=grouped)
+
+        w_grouped, g_grouped, g_codes, g_scales = {}, {}, {}, {}
+        dh, da, da_grouped, da_codes, da_scales = {}, {}, {}, {}, {}
+
+        def turn_x(e):
+            bank = misc_psum.tile([P, PACK, K], F32, name="misc_bank")
+            for t in range(PACK):
+                nc.tensor.transpose(bank[:, t, :], x_slots[:, e * C + t:(e + 1) * C:PACK], ident[:])
+            nc.scalar.activation(out=x_grouped[:, e, :, :], in_=bank[:].rearrange("p t k -> p k t"), func=COPY)
+
+        def group_w(e):
+            w_grouped[e] = ring.tile([P, H, PACK], BF16, name="w_grouped", align_bytes=64)
+            interleave(w_grouped[e][:], w_raw[e][:])
+
+        def quantize_w(e):
+            quantize(w_codes[e][:], w_scales[e][:], w_grouped[e][:].rearrange("p i j -> p (i j)"), E4M3)
+
+        def group_g(e):
+            g_grouped[e] = ring.tile([P, C, PACK], BF16, name="g_grouped", align_bytes=64)
+            interleave(g_grouped[e][:], g_rows[:, :, e * C:(e + 1) * C])
+
+        def quantize_g(e):
+            g_codes[e] = ring.tile([P, C], U32, name="g_codes", align_bytes=64)
+            g_scales[e] = ring.tile([P, C], U8, name="g_scales", align_bytes=64)
+            quantize(g_codes[e][:], g_scales[e][:], g_grouped[e][:].rearrange("p s j -> p (s j)"), E5M2)
+
+        def first_product(e):
+            for b in range(H // P):
+                dh[e, b] = dh_psum.tile([P, C], F32, name="dh_bank")
+                cols = slice(b * P, (b + 1) * P)
+                nc.tensor.matmul_mx(
+                    out=dh[e, b][:],
+                    lhsT=w_codes[e][:, cols].bitcast(E4M3), lhsT_scale=w_scales[e][:, cols],
+                    rhs=g_codes[e][:].bitcast(E5M2), rhs_scale=g_scales[e][:],
+                    start=True, stop=True,
+                )
+
+        def make_da(e, b):
+            if e not in da:
+                da[e] = ring.tile([P, H // P, C], BF16, name="da", align_bytes=64)
+            nc.vector.scalar_tensor_tensor(
+                out=da[e][:, b, :], in0=a_sb[e][:, b, :], scalar=0.0, in1=dh[e, b][:], op0=MAX, op1=MULT)
+
+        def turn_da(e, lo, hi):
+            if e not in da_grouped:
+                da_grouped[e] = ring.tile([P, H, PACK], BF16, name="da_grouped", align_bytes=64)
+            words = da[e][:].rearrange("p b s -> p (b s)").bitcast(F32)
+            grouped_words = da_grouped[e][:].rearrange("p i t -> p (i t)").bitcast(F32)
+            bank = turn_psum.tile([P, 2, 2, P], F32, name="turn_bank")
+            for b in range(lo, hi):
+                for u in range(2):
+                    nc.tensor.transpose(bank[:, b - lo, u, :], words[:, b * 256 + u:(b + 1) * 256:2], ident[:])
+            nc.scalar.copy(
+                out=grouped_words[:, lo * 256:hi * 256].rearrange("p (h i u) -> p h i u", h=hi - lo, u=2),
+                in_=bank[:, 0:hi - lo, :, :].rearrange("p h u i -> p h i u"),
+            )
+
+        def quantize_da(e, lo, hi):
+            if e not in da_codes:
+                da_codes[e] = ring.tile([P, H], U32, name="da_codes", align_bytes=64)
+                da_scales[e] = ring.tile([P, H], U8, name="da_scales", align_bytes=64)
+            cols = slice(lo * P, hi * P)
+            quantize(da_codes[e][:, cols], da_scales[e][:, cols],
+                     da_grouped[e][:, cols, :].rearrange("p i t -> p (i t)"), E5M2)
+
+        def quantize_x(lo, hi):
+            cols = slice(lo * K, hi * K)
+            quantize(x_codes[:, cols], x_scales[:, cols], x_grouped[:, lo:hi, :, :].rearrange("p e k t -> p (e k t)"), E4M3)
+
+        def gather_x(lo, hi):
+            nc.vector.tensor_copy(x_slots[:, lo:hi], x_win[:].indirect(listed(lo, hi)))
+
+        def second_product(e, pieces):
+            bank = misc_psum.tile([P, PACK, K], F32, name="misc_bank")
+            acc = bank[:].rearrange("p t k -> p (t k)")
+            cols = slice(e * K, (e + 1) * K)
+            nc.tensor.matmul_mx(
+                out=acc,
+                lhsT=x_codes[:, cols].bitcast(E4M3), lhsT_scale=x_scales[:, cols],
+                rhs=da_codes[e][:].bitcast(E5M2), rhs_scale=da_scales[e][:],
+                start=True, stop=True,
+            )
+            result = ring.tile([P, H], F32, name="result")
+            width = H // pieces
+            for piece in range(pieces):
+                part = slice(piece * width, (piece + 1) * width)
+                nc.scalar.activation(out=result[:, part], in_=acc[:, part], func=COPY, scale=2.0)
+                nc.sync.dma_start(out=out[e][:, part], in_=result[:, part])
+
+        make_identity(nc, ident[:])
+        nc.sync.dma_start(offsets[:], offs)
+        nc.sync.dma_start(out=x_win[:], in_=xT)
+        load_gate(0 * C, 2 * C)
+        load_dy(0)
+        load_gate(2 * C, 4 * C)
+        load_dy(1)
+        load_w(0)
+        load_dy(2)
+        load_w(1)
+        load_dy(3)
+        load_a(0)
+        load_w(2)
+        load_w(3)
+        load_a(1)
+        load_a(2)
+        load_a(3)
+        gather_x(0 * C, 2 * C)
+        gather_x(2 * C, 4 * C)
+        turn_x(0)
+        turn_x(1)
+        turn_x(2)
+        turn_x(3)
+        gather_g(0, 0 * C, 2 * C)
+        gather_g(0, 2 * C, 4 * C)
+        gather_g(1, 0 * C, 4 * C)
+        group_w(0)
+        quantize_w(0)
+        gather_g(2, 0 * C, 2 * C)
+        group_w(1)
+        gather_g(3, 0 * C, 1 * C)
+        group_g(0)
+        gather_g(3, 1 * C, 2 * C)
+        quantize_w(1)
+        group_g(1)
+        gather_g(2, 2 * C, 4 * C)
+        quantize_g(0)
+        first_product(0)
+        group_w(2)
+        gather_g(3, 2 * C, 3 * C)
+        quantize_g(1)
+        group_g(2)
+        make_da(0, 0)
+        make_da(0, 1)
+        turn_da(0, 0, 2)
+        make_da(0, 2)
+        make_da(0, 3)
+        turn_da(0, 2, 4)
+        first_product(1)
+        gather_g(3, 3 * C, 4 * C)
+        group_w(3)
+        group_g(3)
+        quantize_w(2)
+        make_da(1, 0)
+        make_da(1, 1)
+        turn_da(1, 0, 2)
+        make_da(1, 2)
+        make_da(1, 3)
+        turn_da(1, 2, 4)
+        quantize_da(0, 0, 4)
+        quantize_x(0, 2)
+        second_product(0, 1)
+        quantize_g(2)
+        first_product(2)
+        quantize_w(3)
+        quantize_g(3)
+        make_da(2, 0)
+        make_da(2, 1)
+        turn_da(2, 0, 2)
+        make_da(2, 2)
+        make_da(2, 3)
+        turn_da(2, 2, 4)
+        first_product(3)
+        quantize_da(1, 0, 4)
+        second_product(1, 1)
+        make_da(3, 0)
+        make_da(3, 1)
+        turn_da(3, 0, 2)
+        make_da(3, 2)
+        turn_da(3, 2, 3)
+        make_da(3, 3)
+        turn_da(3, 3, 4)
+        quantize_da(2, 0, 4)
+        quantize_x(2, 4)
+        second_product(2, 1)
+        quantize_da(3, 0, 2)
+        quantize_da(3, 2, 3)
+        quantize_da(3, 3, 4)
+        second_product(3, 2)

@@ -8,6 +8,7 @@ S = E * C
 P = 128
 PACK = 4
 LIST_COL = 16
+GATE_COLS = S // P
 
 FLOPS = 2 * S * N * H + 2 * S * K * H
 BYTES = 4 * (K * T + N * T + H * S + E * N * H + S + E * K * H) + 2 * P * (S // LIST_COL)
@@ -39,6 +40,7 @@ def tile_moe_mlp_relu2_kernel(tc, xT, dyT, a, w2, gate, offs, out):
         gate_sb = keep.tile([P, S], F32, name="gate_sb")
         w_raw = [keep.tile([P, PACK, H], F32, name="w_raw%d" % e) for e in range(E)]
         a_sb = [keep.tile([P, H // P, C], F32, name="a_sb%d" % e) for e in range(E)]
+        gate_col = keep.tile([P, GATE_COLS], F32, name="gate_col")
         x_slots = keep.tile([P, S], F32, name="x_slots")
         g_rows = keep.tile([P, PACK, S], F32, name="g_rows")
         ident = keep.tile([P, P], F32, name="ident")
@@ -54,8 +56,15 @@ def tile_moe_mlp_relu2_kernel(tc, xT, dyT, a, w2, gate, offs, out):
         def load_dy(j):
             nc.sync.dma_start(out=dy_win[j][:], in_=dy_rows[j])
 
-        def load_gate(lo, hi):
-            nc.sync.dma_start(out=gate_sb[:, lo:hi], in_=gate[0:P, lo:hi])
+        def spread_gate():
+            for q in range(GATE_COLS // PACK):
+                bank = dh_psum.tile([P, C], F32, name="dh_bank")
+                for m in range(PACK):
+                    col = q * PACK + m
+                    nc.tensor.transpose(bank[:, m * P:(m + 1) * P], gate_col[:, col:col + 1].to_broadcast([P, P]), ident[:])
+                nc.scalar.activation(
+                    out=gate_sb[:].rearrange("p (n q m) -> p q n m", q=GATE_COLS // PACK, m=PACK)[:, q, :, :],
+                    in_=bank[:].rearrange("p (m n) -> p n m", m=PACK), func=COPY)
 
         def load_w(e):
             nc.sync.dma_start(out=w_raw[e][:], in_=w2[e].rearrange("(p j) i -> p j i", j=PACK))
@@ -88,7 +97,7 @@ def tile_moe_mlp_relu2_kernel(tc, xT, dyT, a, w2, gate, offs, out):
             nc.scalar.activation(out=x_grouped[:, e, :, :], in_=bank[:].rearrange("p t k -> p k t"), func=COPY)
 
         def group_w(e):
-            w_grouped[e] = ring.tile([P, H, PACK], BF16, name="w_grouped", align_bytes=64)
+            w_grouped[e] = ring.tile([P, H, PACK], BF16, name="w_grouped", align_bytes=64, bufs=3)
             interleave(w_grouped[e][:], w_raw[e][:])
 
         def quantize_w(e):
@@ -167,30 +176,29 @@ def tile_moe_mlp_relu2_kernel(tc, xT, dyT, a, w2, gate, offs, out):
                 nc.sync.dma_start(out=out[e][:, part], in_=result[:, part])
 
         make_identity(nc, ident[:])
+        nc.scalar.dma_start(out=gate_col[:], in_=gate[0].rearrange("(p m) -> p m", m=GATE_COLS))
         nc.sync.dma_start(offsets[:], offs)
         nc.sync.dma_start(out=x_win[:], in_=xT)
-        load_gate(0 * C, 2 * C)
         load_dy(0)
-        load_gate(2 * C, 4 * C)
-        load_dy(1)
         load_w(0)
-        load_dy(2)
+        load_dy(1)
         load_w(1)
+        load_dy(2)
+        load_w(2)
         load_dy(3)
         load_a(0)
-        load_w(2)
         load_w(3)
         load_a(1)
         load_a(2)
         load_a(3)
+        spread_gate()
         gather_x(0 * C, 2 * C)
         gather_x(2 * C, 4 * C)
         turn_x(0)
         turn_x(1)
         turn_x(2)
         turn_x(3)
-        gather_g(0, 0 * C, 2 * C)
-        gather_g(0, 2 * C, 4 * C)
+        gather_g(0, 0 * C, 4 * C)
         gather_g(1, 0 * C, 4 * C)
         group_w(0)
         quantize_w(0)

@@ -31,8 +31,7 @@ def tile_moe_mlp_relu2_kernel(tc, xT, dyT, a, w2, gate, offs, out):
         keep = ctx.enter_context(tc.tile_pool(name="keep", bufs=1))
         ring = ctx.enter_context(tc.tile_pool(name="ring", bufs=2))
         dh_psum = ctx.enter_context(tc.psum_pool(name="dh_psum", bufs=4))
-        turn_psum = ctx.enter_context(tc.psum_pool(name="turn_psum", bufs=2))
-        misc_psum = ctx.enter_context(tc.psum_pool(name="misc_psum", bufs=2))
+        work_psum = ctx.enter_context(tc.psum_pool(name="work_psum", bufs=4))
 
         offsets = keep.tile([P, S // LIST_COL], U16, name="offsets")
         x_win = keep.tile([P, T], F32, name="x_win")
@@ -91,13 +90,13 @@ def tile_moe_mlp_relu2_kernel(tc, xT, dyT, a, w2, gate, offs, out):
         dh, da, da_grouped, da_codes, da_scales = {}, {}, {}, {}, {}
 
         def turn_x(e):
-            bank = misc_psum.tile([P, PACK, K], F32, name="misc_bank")
+            bank = work_psum.tile([P, PACK, K], F32, name="work_bank")
             for t in range(PACK):
                 nc.tensor.transpose(bank[:, t, :], x_slots[:, e * C + t:(e + 1) * C:PACK], ident[:])
             nc.scalar.activation(out=x_grouped[:, e, :, :], in_=bank[:].rearrange("p t k -> p k t"), func=COPY)
 
         def group_w(e):
-            w_grouped[e] = ring.tile([P, H, PACK], BF16, name="w_grouped", align_bytes=64, bufs=3)
+            w_grouped[e] = ring.tile([P, H, PACK], BF16, name="staged", align_bytes=64, bufs=4)
             interleave(w_grouped[e][:], w_raw[e][:])
 
         def quantize_w(e):
@@ -131,10 +130,10 @@ def tile_moe_mlp_relu2_kernel(tc, xT, dyT, a, w2, gate, offs, out):
 
         def turn_da(e, lo, hi):
             if e not in da_grouped:
-                da_grouped[e] = ring.tile([P, H, PACK], BF16, name="da_grouped", align_bytes=64)
+                da_grouped[e] = ring.tile([P, H, PACK], BF16, name="staged", align_bytes=64, bufs=4)
             words = da[e][:].rearrange("p b s -> p (b s)").bitcast(F32)
             grouped_words = da_grouped[e][:].rearrange("p i t -> p (i t)").bitcast(F32)
-            bank = turn_psum.tile([P, 2, 2, P], F32, name="turn_bank")
+            bank = work_psum.tile([P, 2, 2, P], F32, name="work_bank")
             for b in range(lo, hi):
                 for u in range(2):
                     nc.tensor.transpose(bank[:, b - lo, u, :], words[:, b * 256 + u:(b + 1) * 256:2], ident[:])
@@ -145,8 +144,8 @@ def tile_moe_mlp_relu2_kernel(tc, xT, dyT, a, w2, gate, offs, out):
 
         def quantize_da(e, lo, hi):
             if e not in da_codes:
-                da_codes[e] = ring.tile([P, H], U32, name="da_codes", align_bytes=64)
-                da_scales[e] = ring.tile([P, H], U8, name="da_scales", align_bytes=64)
+                da_codes[e] = ring.tile([P, H], U32, name="da_codes", align_bytes=64, bufs=3)
+                da_scales[e] = ring.tile([P, H], U8, name="da_scales", align_bytes=64, bufs=3)
             cols = slice(lo * P, hi * P)
             quantize(da_codes[e][:, cols], da_scales[e][:, cols],
                      da_grouped[e][:, cols, :].rearrange("p i t -> p (i t)"), E5M2)
@@ -159,7 +158,7 @@ def tile_moe_mlp_relu2_kernel(tc, xT, dyT, a, w2, gate, offs, out):
             nc.vector.tensor_copy(x_slots[:, lo:hi], x_win[:].indirect(listed(lo, hi)))
 
         def second_product(e, pieces):
-            bank = misc_psum.tile([P, PACK, K], F32, name="misc_bank")
+            bank = work_psum.tile([P, PACK, K], F32, name="work_bank")
             acc = bank[:].rearrange("p t k -> p (t k)")
             cols = slice(e * K, (e + 1) * K)
             nc.tensor.matmul_mx(
@@ -168,7 +167,7 @@ def tile_moe_mlp_relu2_kernel(tc, xT, dyT, a, w2, gate, offs, out):
                 rhs=da_codes[e][:].bitcast(E5M2), rhs_scale=da_scales[e][:],
                 start=True, stop=True,
             )
-            result = ring.tile([P, H], F32, name="result")
+            result = ring.tile([P, H], F32, name="result", bufs=4)
             width = H // pieces
             for piece in range(pieces):
                 part = slice(piece * width, (piece + 1) * width)
@@ -185,9 +184,9 @@ def tile_moe_mlp_relu2_kernel(tc, xT, dyT, a, w2, gate, offs, out):
         load_w(1)
         load_dy(2)
         load_w(2)
+        load_w(3)
         load_dy(3)
         load_a(0)
-        load_w(3)
         load_a(1)
         load_a(2)
         load_a(3)
@@ -199,23 +198,27 @@ def tile_moe_mlp_relu2_kernel(tc, xT, dyT, a, w2, gate, offs, out):
         turn_x(2)
         turn_x(3)
         gather_g(0, 0 * C, 4 * C)
-        gather_g(1, 0 * C, 4 * C)
         group_w(0)
-        quantize_w(0)
-        gather_g(2, 0 * C, 2 * C)
+        gather_g(1, 0 * C, 4 * C)
         group_w(1)
+        quantize_w(0)
+        gather_g(2, 0 * C, 4 * C)
+        group_w(2)
+        quantize_w(1)
+        quantize_x(0, 4)
+        group_w(3)
+        quantize_w(2)
         gather_g(3, 0 * C, 1 * C)
         group_g(0)
         gather_g(3, 1 * C, 2 * C)
-        quantize_w(1)
         group_g(1)
-        gather_g(2, 2 * C, 4 * C)
+        gather_g(3, 2 * C, 3 * C)
+        quantize_w(3)
         quantize_g(0)
         first_product(0)
-        group_w(2)
-        gather_g(3, 2 * C, 3 * C)
-        quantize_g(1)
         group_g(2)
+        gather_g(3, 3 * C, 4 * C)
+        quantize_g(1)
         make_da(0, 0)
         make_da(0, 1)
         turn_da(0, 0, 2)
@@ -223,22 +226,15 @@ def tile_moe_mlp_relu2_kernel(tc, xT, dyT, a, w2, gate, offs, out):
         make_da(0, 3)
         turn_da(0, 2, 4)
         first_product(1)
-        gather_g(3, 3 * C, 4 * C)
-        group_w(3)
         group_g(3)
-        quantize_w(2)
+        quantize_g(2)
         make_da(1, 0)
         make_da(1, 1)
         turn_da(1, 0, 2)
         make_da(1, 2)
         make_da(1, 3)
         turn_da(1, 2, 4)
-        quantize_da(0, 0, 4)
-        quantize_x(0, 2)
-        second_product(0, 1)
-        quantize_g(2)
         first_product(2)
-        quantize_w(3)
         quantize_g(3)
         make_da(2, 0)
         make_da(2, 1)
@@ -247,8 +243,8 @@ def tile_moe_mlp_relu2_kernel(tc, xT, dyT, a, w2, gate, offs, out):
         make_da(2, 3)
         turn_da(2, 2, 4)
         first_product(3)
-        quantize_da(1, 0, 4)
-        second_product(1, 1)
+        quantize_da(0, 0, 4)
+        second_product(0, 1)
         make_da(3, 0)
         make_da(3, 1)
         turn_da(3, 0, 2)
@@ -256,8 +252,9 @@ def tile_moe_mlp_relu2_kernel(tc, xT, dyT, a, w2, gate, offs, out):
         turn_da(3, 2, 3)
         make_da(3, 3)
         turn_da(3, 3, 4)
+        quantize_da(1, 0, 4)
+        second_product(1, 1)
         quantize_da(2, 0, 4)
-        quantize_x(2, 4)
         second_product(2, 1)
         quantize_da(3, 0, 2)
         quantize_da(3, 2, 3)

@@ -7,8 +7,11 @@ K, T, E, C, H, N = 128, 2560, 4, 512, 512, 512
 S = E * C
 P = 128
 PACK = 4
+BLOCKS = H // P
 LIST_COL = 16
 GATE_COLS = S // P
+RUN = 4
+PAIRS = C // 2
 
 FLOPS = 2 * S * N * H + 2 * S * K * H
 BYTES = 4 * (K * T + N * T + H * S + E * N * H + S + E * K * H) + 2 * P * (S // LIST_COL)
@@ -27,236 +30,204 @@ COPY = mybir.ActivationFunctionType.Copy
 
 def tile_moe_mlp_relu2_kernel(tc, xT, dyT, a, w2, gate, offs, out):
     nc = tc.nc
+    last = E - 1
     with ExitStack() as ctx:
         keep = ctx.enter_context(tc.tile_pool(name="keep", bufs=1))
         ring = ctx.enter_context(tc.tile_pool(name="ring", bufs=2))
-        dh_psum = ctx.enter_context(tc.psum_pool(name="dh_psum", bufs=4))
+        dh_psum = ctx.enter_context(tc.psum_pool(name="dh_psum", bufs=BLOCKS))
         work_psum = ctx.enter_context(tc.psum_pool(name="work_psum", bufs=4))
 
         offsets = keep.tile([P, S // LIST_COL], U16, name="offsets")
-        x_win = keep.tile([P, T], F32, name="x_win")
-        dy_win = [keep.tile([P, T], F32, name="dy_win%d" % j) for j in range(PACK)]
-        gate_sb = keep.tile([P, S], F32, name="gate_sb")
-        w_raw = [keep.tile([P, PACK, H], F32, name="w_raw%d" % e) for e in range(E)]
-        a_sb = [keep.tile([P, H // P, C], F32, name="a_sb%d" % e) for e in range(E)]
+        x_window = keep.tile([P, T], F32, name="x_window")
+        dy_window = [keep.tile([P, T], F32, name="dy_window%d" % t) for t in range(PACK)]
         gate_col = keep.tile([P, GATE_COLS], F32, name="gate_col")
-        x_slots = keep.tile([P, S], F32, name="x_slots")
+        gate_row = keep.tile([P, S], F32, name="gate_row")
+        w_rows = [keep.tile([P, PACK, H], F32, name="w_rows%d" % e) for e in range(E)]
+        a_rows = [keep.tile([P, BLOCKS, C], F32, name="a_rows%d" % e) for e in range(E)]
         g_rows = keep.tile([P, PACK, S], F32, name="g_rows")
         ident = keep.tile([P, P], F32, name="ident")
-        x_grouped = keep.tile([P, E, K, PACK], BF16, name="x_grouped", align_bytes=64)
-        x_codes = keep.tile([P, E * K], U32, name="x_codes", align_bytes=64)
-        x_scales = keep.tile([P, E * K], U8, name="x_scales", align_bytes=64)
-        w_codes = [keep.tile([P, H], U32, name="w_codes%d" % e, align_bytes=64) for e in range(E)]
-        w_scales = [keep.tile([P, H], U8, name="w_scales%d" % e, align_bytes=64) for e in range(E)]
+        x_slots = keep.tile([P, S], F32, name="x_slots", tag="slots_then_results")
+        results = keep.tile([P, E, H], F32, name="results", tag="slots_then_results")
 
-        dy_rows = dyT.rearrange("(p j) t -> j p t", j=PACK)
-        a_rows = a.rearrange("(b p) s -> p b s", p=P)
+        xw_grouped = keep.tile([P, (1 + E) * H, PACK], BF16, name="xw_grouped", tag="xw_then_da", align_bytes=64)
+        xw_codes = keep.tile([P, E * H], U32, name="xw_codes", align_bytes=64)
+        xw_scales = keep.tile([P, (1 + E) * H], U8, name="xw_scales", align_bytes=64)
+        g_grouped = [keep.tile([P, C, PACK], BF16, name="g_grouped%d" % e, tag="after_g%d" % e, align_bytes=64) for e in range(E)]
+        last_w_codes = keep.tile([P, H], U32, name="last_w_codes", tag="after_g0", align_bytes=64)
+        da = [keep.tile([P, BLOCKS, C], BF16, name="da%d" % e, tag="after_g%d" % (e + 1), align_bytes=64) for e in range(E)]
+        da_grouped = keep.tile([P, E * H, PACK], BF16, name="da_grouped", tag="xw_then_da", align_bytes=64)
+        da_codes = keep.tile([P, E * H], U32, name="da_codes", align_bytes=64)
+        da_scales = keep.tile([P, E * H], U8, name="da_scales", align_bytes=64)
+        g_codes, g_scales, dh = {}, {}, {}
 
-        def load_dy(j):
-            nc.sync.dma_start(out=dy_win[j][:], in_=dy_rows[j])
-
-        def spread_gate():
-            for q in range(GATE_COLS // PACK):
-                bank = dh_psum.tile([P, C], F32, name="dh_bank")
-                for m in range(PACK):
-                    col = q * PACK + m
-                    nc.tensor.transpose(bank[:, m * P:(m + 1) * P], gate_col[:, col:col + 1].to_broadcast([P, P]), ident[:])
-                nc.scalar.activation(
-                    out=gate_sb[:].rearrange("p (n q m) -> p q n m", q=GATE_COLS // PACK, m=PACK)[:, q, :, :],
-                    in_=bank[:].rearrange("p (m n) -> p n m", m=PACK), func=COPY)
+        def load_dy(t, lo, hi):
+            rows = dyT.rearrange("(p t) token -> t p token", t=PACK)[t]
+            nc.sync.dma_start(out=dy_window[t][:, lo:hi], in_=rows[:, lo:hi])
 
         def load_w(e):
-            nc.sync.dma_start(out=w_raw[e][:], in_=w2[e].rearrange("(p j) i -> p j i", j=PACK))
+            nc.sync.dma_start(out=w_rows[e][:], in_=w2[e].rearrange("(p t) i -> p t i", t=PACK))
 
         def load_a(e):
-            nc.sync.dma_start(out=a_sb[e][:], in_=a_rows[:, :, e * C:(e + 1) * C])
+            nc.sync.dma_start(out=a_rows[e][:], in_=a.rearrange("(b p) j -> p b j", p=P)[:, :, e * C:(e + 1) * C])
+
+        def spread_gate():
+            quads = GATE_COLS // PACK
+            for q in range(quads):
+                bank = dh_psum.tile([P, C], F32, name="dh_bank")
+                for r in range(PACK):
+                    m = q * PACK + r
+                    nc.tensor.transpose(bank[:, r * P:(r + 1) * P], gate_col[:, m:m + 1].to_broadcast([P, P]), ident[:])
+                nc.scalar.activation(
+                    out=gate_row[:].rearrange("p (n q r) -> p q n r", q=quads, r=PACK)[:, q, :, :],
+                    in_=bank[:].rearrange("p (r n) -> p n r", r=PACK), func=COPY)
 
         def listed(lo, hi):
             return offsets[:, lo // LIST_COL:hi // LIST_COL]
 
-        def gather_g(j, lo, hi):
-            nc.vector.tensor_tensor(g_rows[:, j, lo:hi], dy_win[j][:].indirect(listed(lo, hi)), gate_sb[:, lo:hi], MULT)
+        def gather_x(lo, hi):
+            nc.vector.tensor_copy(x_slots[:, lo:hi], x_window[:].indirect(listed(lo, hi)))
 
-        def interleave(dst, src):
+        def gather_g(t, lo, hi):
+            nc.vector.tensor_tensor(g_rows[:, t, lo:hi], dy_window[t][:].indirect(listed(lo, hi)), gate_row[:, lo:hi], MULT)
+
+        def group(grouped, rows):
             nc.scalar.copy(
-                out=dst.rearrange("p (c i) j -> p c j i", i=4),
-                in_=src.rearrange("p j (c i) -> p c j i", i=4),
-            )
+                out=grouped.rearrange("p (c r) t -> p c t r", r=RUN),
+                in_=rows.rearrange("p t (c r) -> p c t r", r=RUN))
 
-        def quantize(codes, scales, grouped, fmt):
-            nc.vector.quantize_mx(out=codes.bitcast(fmt), scales=scales, in_=grouped)
+        def group_w(e):
+            group(xw_grouped[:, (1 + e) * H:(2 + e) * H, :], w_rows[e][:])
 
-        w_grouped, g_grouped, g_codes, g_scales = {}, {}, {}, {}
-        dh, da, da_grouped, da_codes, da_scales = {}, {}, {}, {}, {}
+        def group_g(e):
+            group(g_grouped[e][:], g_rows[:, :, e * C:(e + 1) * C])
 
         def turn_x(e):
             bank = work_psum.tile([P, PACK, K], F32, name="work_bank")
             for t in range(PACK):
                 nc.tensor.transpose(bank[:, t, :], x_slots[:, e * C + t:(e + 1) * C:PACK], ident[:])
-            nc.scalar.activation(out=x_grouped[:, e, :, :], in_=bank[:].rearrange("p t k -> p k t"), func=COPY)
+            nc.scalar.activation(out=xw_grouped[:, e * K:(e + 1) * K, :], in_=bank[:].rearrange("p t k -> p k t"), func=COPY)
 
-        def group_w(e):
-            w_grouped[e] = ring.tile([P, H, PACK], BF16, name="staged", align_bytes=64, bufs=4)
-            interleave(w_grouped[e][:], w_raw[e][:])
+        def quantize(codes, scales, grouped, fmt):
+            nc.vector.quantize_mx(out=codes.bitcast(fmt), scales=scales, in_=grouped.rearrange("p c t -> p (c t)"))
 
-        def quantize_w(e):
-            quantize(w_codes[e][:], w_scales[e][:], w_grouped[e][:].rearrange("p i j -> p (i j)"), E4M3)
+        def quantize_xw(lo, hi):
+            cols = slice(lo * H, hi * H)
+            quantize(xw_codes[:, cols], xw_scales[:, cols], xw_grouped[:, cols, :], E4M3)
 
-        def group_g(e):
-            g_grouped[e] = ring.tile([P, C, PACK], BF16, name="g_grouped", align_bytes=64)
-            interleave(g_grouped[e][:], g_rows[:, :, e * C:(e + 1) * C])
+        def quantize_last_w():
+            cols = slice(E * H, (1 + E) * H)
+            quantize(last_w_codes[:], xw_scales[:, cols], xw_grouped[:, cols, :], E4M3)
 
         def quantize_g(e):
             g_codes[e] = ring.tile([P, C], U32, name="g_codes", align_bytes=64)
             g_scales[e] = ring.tile([P, C], U8, name="g_scales", align_bytes=64)
-            quantize(g_codes[e][:], g_scales[e][:], g_grouped[e][:].rearrange("p s j -> p (s j)"), E5M2)
+            quantize(g_codes[e][:], g_scales[e][:], g_grouped[e][:], E5M2)
 
         def first_product(e):
-            for b in range(H // P):
+            section = slice((1 + e) * H, (2 + e) * H)
+            w_codes = last_w_codes[:] if e == last else xw_codes[:, section]
+            w_scales = xw_scales[:, section]
+            for b in range(BLOCKS):
                 dh[e, b] = dh_psum.tile([P, C], F32, name="dh_bank")
                 cols = slice(b * P, (b + 1) * P)
                 nc.tensor.matmul_mx(
                     out=dh[e, b][:],
-                    lhsT=w_codes[e][:, cols].bitcast(E4M3), lhsT_scale=w_scales[e][:, cols],
+                    lhsT=w_codes[:, cols].bitcast(E4M3), lhsT_scale=w_scales[:, cols],
                     rhs=g_codes[e][:].bitcast(E5M2), rhs_scale=g_scales[e][:],
-                    start=True, stop=True,
-                )
+                    start=True, stop=True)
 
-        def make_da(e, b):
-            if e not in da:
-                da[e] = ring.tile([P, H // P, C], BF16, name="da", align_bytes=64)
-            nc.vector.scalar_tensor_tensor(
-                out=da[e][:, b, :], in0=a_sb[e][:, b, :], scalar=0.0, in1=dh[e, b][:], op0=MAX, op1=MULT)
+        def make_da(e):
+            for b in range(BLOCKS):
+                nc.vector.scalar_tensor_tensor(
+                    out=da[e][:, b, :], in0=a_rows[e][:, b, :], scalar=0.0, in1=dh[e, b][:], op0=MAX, op1=MULT)
 
         def turn_da(e, lo, hi):
-            if e not in da_grouped:
-                da_grouped[e] = ring.tile([P, H, PACK], BF16, name="staged", align_bytes=64, bufs=4)
-            words = da[e][:].rearrange("p b s -> p (b s)").bitcast(F32)
-            grouped_words = da_grouped[e][:].rearrange("p i t -> p (i t)").bitcast(F32)
+            words = da[e][:].rearrange("p b c -> p (b c)").bitcast(F32)
+            grouped_words = da_grouped[:, e * H + lo * P:e * H + hi * P, :].rearrange("p i t -> p (i t)").bitcast(F32)
             bank = work_psum.tile([P, 2, 2, P], F32, name="work_bank")
             for b in range(lo, hi):
                 for u in range(2):
-                    nc.tensor.transpose(bank[:, b - lo, u, :], words[:, b * 256 + u:(b + 1) * 256:2], ident[:])
+                    nc.tensor.transpose(bank[:, b - lo, u, :], words[:, b * PAIRS + u:(b + 1) * PAIRS:2], ident[:])
             nc.scalar.copy(
-                out=grouped_words[:, lo * 256:hi * 256].rearrange("p (h i u) -> p h i u", h=hi - lo, u=2),
-                in_=bank[:, 0:hi - lo, :, :].rearrange("p h u i -> p h i u"),
-            )
+                out=grouped_words.rearrange("p (b i u) -> p b i u", b=hi - lo, u=2),
+                in_=bank[:, 0:hi - lo, :, :].rearrange("p b u i -> p b i u"))
 
         def quantize_da(e, lo, hi):
-            if e not in da_codes:
-                da_codes[e] = ring.tile([P, H], U32, name="da_codes", align_bytes=64, bufs=3)
-                da_scales[e] = ring.tile([P, H], U8, name="da_scales", align_bytes=64, bufs=3)
-            cols = slice(lo * P, hi * P)
-            quantize(da_codes[e][:, cols], da_scales[e][:, cols],
-                     da_grouped[e][:, cols, :].rearrange("p i t -> p (i t)"), E5M2)
-
-        def quantize_x(lo, hi):
-            cols = slice(lo * K, hi * K)
-            quantize(x_codes[:, cols], x_scales[:, cols], x_grouped[:, lo:hi, :, :].rearrange("p e k t -> p (e k t)"), E4M3)
-
-        def gather_x(lo, hi):
-            nc.vector.tensor_copy(x_slots[:, lo:hi], x_win[:].indirect(listed(lo, hi)))
+            cols = slice(e * H + lo * P, e * H + hi * P)
+            quantize(da_codes[:, cols], da_scales[:, cols], da_grouped[:, cols, :], E5M2)
 
         def second_product(e, pieces):
-            bank = work_psum.tile([P, PACK, K], F32, name="work_bank")
-            acc = bank[:].rearrange("p t k -> p (t k)")
-            cols = slice(e * K, (e + 1) * K)
+            bank = work_psum.tile([P, H], F32, name="work_bank")
+            x_cols = slice(e * K, (e + 1) * K)
+            da_cols = slice(e * H, (e + 1) * H)
             nc.tensor.matmul_mx(
-                out=acc,
-                lhsT=x_codes[:, cols].bitcast(E4M3), lhsT_scale=x_scales[:, cols],
-                rhs=da_codes[e][:].bitcast(E5M2), rhs_scale=da_scales[e][:],
-                start=True, stop=True,
-            )
-            result = ring.tile([P, H], F32, name="result", bufs=4)
+                out=bank[:],
+                lhsT=xw_codes[:, x_cols].bitcast(E4M3), lhsT_scale=xw_scales[:, x_cols],
+                rhs=da_codes[:, da_cols].bitcast(E5M2), rhs_scale=da_scales[:, da_cols],
+                start=True, stop=True)
             width = H // pieces
             for piece in range(pieces):
                 part = slice(piece * width, (piece + 1) * width)
-                nc.scalar.activation(out=result[:, part], in_=acc[:, part], func=COPY, scale=2.0)
-                nc.sync.dma_start(out=out[e][:, part], in_=result[:, part])
+                nc.scalar.activation(out=results[:, e, part], in_=bank[:, part], func=COPY, scale=2.0)
+                nc.sync.dma_start(out=out[e][:, part], in_=results[:, e, part])
 
         make_identity(nc, ident[:])
+
         nc.scalar.dma_start(out=gate_col[:], in_=gate[0].rearrange("(p m) -> p m", m=GATE_COLS))
         nc.sync.dma_start(offsets[:], offs)
-        nc.sync.dma_start(out=x_win[:], in_=xT)
-        load_dy(0)
+        nc.sync.dma_start(out=x_window[:], in_=xT)
+        load_dy(0, 0, T)
+        load_dy(1, 0, T)
         load_w(0)
-        load_dy(1)
+        load_dy(2, 0, T)
         load_w(1)
-        load_dy(2)
         load_w(2)
+        load_dy(3, 0, T // 2)
         load_w(3)
-        load_dy(3)
-        load_a(0)
-        load_a(1)
-        load_a(2)
-        load_a(3)
+        load_dy(3, T // 2, T)
+        for e in range(E):
+            load_a(e)
+
         spread_gate()
-        gather_x(0 * C, 2 * C)
-        gather_x(2 * C, 4 * C)
-        turn_x(0)
-        turn_x(1)
-        turn_x(2)
-        turn_x(3)
-        gather_g(0, 0 * C, 4 * C)
+        gather_x(0, S // 2)
+        gather_x(S // 2, S)
+        for e in range(E):
+            turn_x(e)
+        gather_g(0, 0, S)
+        gather_g(1, 0, S)
         group_w(0)
-        gather_g(1, 0 * C, 4 * C)
+        quantize_xw(0, 2)
+        gather_g(2, 0, S)
         group_w(1)
-        quantize_w(0)
-        gather_g(2, 0 * C, 4 * C)
         group_w(2)
-        quantize_w(1)
-        quantize_x(0, 4)
+        quantize_xw(2, 4)
         group_w(3)
-        quantize_w(2)
-        gather_g(3, 0 * C, 1 * C)
-        group_g(0)
-        gather_g(3, 1 * C, 2 * C)
-        group_g(1)
-        gather_g(3, 2 * C, 3 * C)
-        quantize_w(3)
+        for e in range(E):
+            gather_g(3, e * C, (e + 1) * C)
+            group_g(e)
+
         quantize_g(0)
         first_product(0)
-        group_g(2)
-        gather_g(3, 3 * C, 4 * C)
-        quantize_g(1)
-        make_da(0, 0)
-        make_da(0, 1)
-        turn_da(0, 0, 2)
-        make_da(0, 2)
-        make_da(0, 3)
-        turn_da(0, 2, 4)
-        first_product(1)
-        group_g(3)
-        quantize_g(2)
-        make_da(1, 0)
-        make_da(1, 1)
-        turn_da(1, 0, 2)
-        make_da(1, 2)
-        make_da(1, 3)
-        turn_da(1, 2, 4)
-        first_product(2)
-        quantize_g(3)
-        make_da(2, 0)
-        make_da(2, 1)
-        turn_da(2, 0, 2)
-        make_da(2, 2)
-        make_da(2, 3)
-        turn_da(2, 2, 4)
-        first_product(3)
-        quantize_da(0, 0, 4)
+        quantize_last_w()
+        for e in range(last):
+            quantize_g(e + 1)
+            if e > 0:
+                turn_da(e - 1, 0, 2)
+                turn_da(e - 1, 2, 4)
+            make_da(e)
+            first_product(e + 1)
+        quantize_da(0, 0, BLOCKS)
+        turn_da(last - 1, 0, 2)
+        turn_da(last - 1, 2, 4)
         second_product(0, 1)
-        make_da(3, 0)
-        make_da(3, 1)
-        turn_da(3, 0, 2)
-        make_da(3, 2)
-        turn_da(3, 2, 3)
-        make_da(3, 3)
-        turn_da(3, 3, 4)
-        quantize_da(1, 0, 4)
-        second_product(1, 1)
-        quantize_da(2, 0, 4)
-        second_product(2, 1)
-        quantize_da(3, 0, 2)
-        quantize_da(3, 2, 3)
-        quantize_da(3, 3, 4)
-        second_product(3, 2)
+
+        parts = [(0, 2), (2, 3), (3, 4)]
+        make_da(last)
+        for lo, hi in parts:
+            turn_da(last, lo, hi)
+        for e in range(1, last):
+            quantize_da(e, 0, BLOCKS)
+            second_product(e, 1)
+        for lo, hi in parts:
+            quantize_da(last, lo, hi)
+        second_product(last, 2)

from contextlib import ExitStack

import concourse.mybir as mybir
from concourse.masks import make_identity

K, T, E, C, H, N = 128, 2560, 4, 512, 512, 512
S = E * C
P = 128
PACK = 4
BLOCKS = H // P
LIST_COL = 16
GATE_COLS = S // P
RUN = 4
PAIRS = C // 2

FLOPS = 2 * S * N * H + 2 * S * K * H
BYTES = 4 * (K * T + N * T + H * S + E * N * H + S + E * K * H) + 2 * P * (S // LIST_COL)

F32 = mybir.dt.float32
BF16 = mybir.dt.bfloat16
U32 = mybir.dt.uint32
U16 = mybir.dt.uint16
U8 = mybir.dt.uint8
E4M3 = mybir.dt.float8_e4m3fn_x4
E5M2 = mybir.dt.float8_e5m2_x4
MULT = mybir.AluOpType.mult
MAX = mybir.AluOpType.max
COPY = mybir.ActivationFunctionType.Copy


def tile_moe_mlp_relu2_kernel(tc, xT, dyT, a, w2, gate, offs, out):
    nc = tc.nc
    last = E - 1
    with ExitStack() as ctx:
        keep = ctx.enter_context(tc.tile_pool(name="keep", bufs=1))
        ring = ctx.enter_context(tc.tile_pool(name="ring", bufs=2))
        dh_psum = ctx.enter_context(tc.psum_pool(name="dh_psum", bufs=BLOCKS))
        work_psum = ctx.enter_context(tc.psum_pool(name="work_psum", bufs=4))

        offsets = keep.tile([P, S // LIST_COL], U16, name="offsets")
        x_window = keep.tile([P, T], F32, name="x_window")
        dy_window = [keep.tile([P, T], F32, name="dy_window%d" % t) for t in range(PACK)]
        gate_col = keep.tile([P, GATE_COLS], F32, name="gate_col")
        gate_row = keep.tile([P, S], F32, name="gate_row")
        w_rows = [keep.tile([P, PACK, H], F32, name="w_rows%d" % e) for e in range(E)]
        a_rows = [keep.tile([P, BLOCKS, C], F32, name="a_rows%d" % e) for e in range(E)]
        g_rows = keep.tile([P, PACK, S], F32, name="g_rows")
        ident = keep.tile([P, P], F32, name="ident")
        x_slots = keep.tile([P, S], F32, name="x_slots", tag="slots_then_results")
        results = keep.tile([P, E, H], F32, name="results", tag="slots_then_results")

        xw_grouped = keep.tile([P, (1 + E) * H, PACK], BF16, name="xw_grouped", tag="xw_then_da", align_bytes=64)
        xw_codes = keep.tile([P, E * H], U32, name="xw_codes", align_bytes=64)
        xw_scales = keep.tile([P, (1 + E) * H], U8, name="xw_scales", align_bytes=64)
        g_grouped = [keep.tile([P, C, PACK], BF16, name="g_grouped%d" % e, tag="after_g%d" % e, align_bytes=64) for e in range(E)]
        last_w_codes = keep.tile([P, H], U32, name="last_w_codes", tag="after_g0", align_bytes=64)
        da = [keep.tile([P, BLOCKS, C], BF16, name="da%d" % e, tag="after_g%d" % (e + 1), align_bytes=64) for e in range(E)]
        da_grouped = keep.tile([P, E * H, PACK], BF16, name="da_grouped", tag="xw_then_da", align_bytes=64)
        da_codes = keep.tile([P, E * H], U32, name="da_codes", align_bytes=64)
        da_scales = keep.tile([P, E * H], U8, name="da_scales", align_bytes=64)
        g_codes, g_scales, dh = {}, {}, {}

        def load_dy(t, lo, hi):
            rows = dyT.rearrange("(p t) token -> t p token", t=PACK)[t]
            nc.sync.dma_start(out=dy_window[t][:, lo:hi], in_=rows[:, lo:hi])

        def load_w(e):
            nc.sync.dma_start(out=w_rows[e][:], in_=w2[e].rearrange("(p t) i -> p t i", t=PACK))

        def load_a(e):
            nc.sync.dma_start(out=a_rows[e][:], in_=a.rearrange("(b p) j -> p b j", p=P)[:, :, e * C:(e + 1) * C])

        def spread_gate():
            quads = GATE_COLS // PACK
            for q in range(quads):
                bank = dh_psum.tile([P, C], F32, name="dh_bank")
                for r in range(PACK):
                    m = q * PACK + r
                    nc.tensor.transpose(bank[:, r * P:(r + 1) * P], gate_col[:, m:m + 1].to_broadcast([P, P]), ident[:])
                nc.scalar.activation(
                    out=gate_row[:].rearrange("p (n q r) -> p q n r", q=quads, r=PACK)[:, q, :, :],
                    in_=bank[:].rearrange("p (r n) -> p n r", r=PACK), func=COPY)

        def listed(lo, hi):
            return offsets[:, lo // LIST_COL:hi // LIST_COL]

        def gather_x(lo, hi):
            nc.vector.tensor_copy(x_slots[:, lo:hi], x_window[:].indirect(listed(lo, hi)))

        def gather_g(t, lo, hi):
            nc.vector.tensor_tensor(g_rows[:, t, lo:hi], dy_window[t][:].indirect(listed(lo, hi)), gate_row[:, lo:hi], MULT)

        def group(grouped, rows):
            nc.scalar.copy(
                out=grouped.rearrange("p (c r) t -> p c t r", r=RUN),
                in_=rows.rearrange("p t (c r) -> p c t r", r=RUN))

        def group_w(e):
            group(xw_grouped[:, (1 + e) * H:(2 + e) * H, :], w_rows[e][:])

        def group_g(e):
            group(g_grouped[e][:], g_rows[:, :, e * C:(e + 1) * C])

        def turn_x(e):
            bank = work_psum.tile([P, PACK, K], F32, name="work_bank")
            for t in range(PACK):
                nc.tensor.transpose(bank[:, t, :], x_slots[:, e * C + t:(e + 1) * C:PACK], ident[:])
            nc.scalar.activation(out=xw_grouped[:, e * K:(e + 1) * K, :], in_=bank[:].rearrange("p t k -> p k t"), func=COPY)

        def quantize(codes, scales, grouped, fmt):
            nc.vector.quantize_mx(out=codes.bitcast(fmt), scales=scales, in_=grouped.rearrange("p c t -> p (c t)"))

        def quantize_xw(lo, hi):
            cols = slice(lo * H, hi * H)
            quantize(xw_codes[:, cols], xw_scales[:, cols], xw_grouped[:, cols, :], E4M3)

        def quantize_last_w():
            cols = slice(E * H, (1 + E) * H)
            quantize(last_w_codes[:], xw_scales[:, cols], xw_grouped[:, cols, :], E4M3)

        def quantize_g(e):
            g_codes[e] = ring.tile([P, C], U32, name="g_codes", align_bytes=64)
            g_scales[e] = ring.tile([P, C], U8, name="g_scales", align_bytes=64)
            quantize(g_codes[e][:], g_scales[e][:], g_grouped[e][:], E5M2)

        def first_product(e):
            section = slice((1 + e) * H, (2 + e) * H)
            w_codes = last_w_codes[:] if e == last else xw_codes[:, section]
            w_scales = xw_scales[:, section]
            for b in range(BLOCKS):
                dh[e, b] = dh_psum.tile([P, C], F32, name="dh_bank")
                cols = slice(b * P, (b + 1) * P)
                nc.tensor.matmul_mx(
                    out=dh[e, b][:],
                    lhsT=w_codes[:, cols].bitcast(E4M3), lhsT_scale=w_scales[:, cols],
                    rhs=g_codes[e][:].bitcast(E5M2), rhs_scale=g_scales[e][:],
                    start=True, stop=True)

        def make_da(e):
            for b in range(BLOCKS):
                nc.vector.scalar_tensor_tensor(
                    out=da[e][:, b, :], in0=a_rows[e][:, b, :], scalar=0.0, in1=dh[e, b][:], op0=MAX, op1=MULT)

        def turn_da(e, lo, hi):
            words = da[e][:].rearrange("p b c -> p (b c)").bitcast(F32)
            grouped_words = da_grouped[:, e * H + lo * P:e * H + hi * P, :].rearrange("p i t -> p (i t)").bitcast(F32)
            bank = work_psum.tile([P, 2, 2, P], F32, name="work_bank")
            for b in range(lo, hi):
                for u in range(2):
                    nc.tensor.transpose(bank[:, b - lo, u, :], words[:, b * PAIRS + u:(b + 1) * PAIRS:2], ident[:])
            nc.scalar.copy(
                out=grouped_words.rearrange("p (b i u) -> p b i u", b=hi - lo, u=2),
                in_=bank[:, 0:hi - lo, :, :].rearrange("p b u i -> p b i u"))

        def quantize_da(e, lo, hi):
            cols = slice(e * H + lo * P, e * H + hi * P)
            quantize(da_codes[:, cols], da_scales[:, cols], da_grouped[:, cols, :], E5M2)

        def second_product(e, pieces):
            bank = work_psum.tile([P, H], F32, name="work_bank")
            x_cols = slice(e * K, (e + 1) * K)
            da_cols = slice(e * H, (e + 1) * H)
            nc.tensor.matmul_mx(
                out=bank[:],
                lhsT=xw_codes[:, x_cols].bitcast(E4M3), lhsT_scale=xw_scales[:, x_cols],
                rhs=da_codes[:, da_cols].bitcast(E5M2), rhs_scale=da_scales[:, da_cols],
                start=True, stop=True)
            width = H // pieces
            for piece in range(pieces):
                part = slice(piece * width, (piece + 1) * width)
                nc.scalar.activation(out=results[:, e, part], in_=bank[:, part], func=COPY, scale=2.0)
                nc.sync.dma_start(out=out[e][:, part], in_=results[:, e, part])

        make_identity(nc, ident[:])

        nc.scalar.dma_start(out=gate_col[:], in_=gate[0].rearrange("(p m) -> p m", m=GATE_COLS))
        nc.sync.dma_start(offsets[:], offs)
        nc.sync.dma_start(out=x_window[:], in_=xT)
        load_dy(0, 0, T)
        load_dy(1, 0, T)
        load_w(0)
        load_dy(2, 0, T)
        load_w(1)
        load_w(2)
        load_dy(3, 0, T // 2)
        load_w(3)
        load_dy(3, T // 2, T)
        for e in range(E):
            load_a(e)

        spread_gate()
        gather_x(0, S // 2)
        gather_x(S // 2, S)
        for e in range(E):
            turn_x(e)
        gather_g(0, 0, S)
        gather_g(1, 0, S)
        group_w(0)
        quantize_xw(0, 2)
        gather_g(2, 0, S)
        group_w(1)
        group_w(2)
        quantize_xw(2, 4)
        group_w(3)
        for e in range(E):
            gather_g(3, e * C, (e + 1) * C)
            group_g(e)

        quantize_g(0)
        first_product(0)
        quantize_last_w()
        for e in range(last):
            quantize_g(e + 1)
            if e > 0:
                turn_da(e - 1, 0, 2)
                turn_da(e - 1, 2, 4)
            make_da(e)
            first_product(e + 1)
        quantize_da(0, 0, BLOCKS)
        turn_da(last - 1, 0, 2)
        turn_da(last - 1, 2, 4)
        second_product(0, 1)

        parts = [(0, 2), (2, 3), (3, 4)]
        make_da(last)
        for lo, hi in parts:
            turn_da(last, lo, hi)
        for e in range(1, last):
            quantize_da(e, 0, BLOCKS)
            second_product(e, 1)
        for lo, hi in parts:
            quantize_da(last, lo, hi)
        second_product(last, 2)
